import numpy as np, ml_dtypes
CORES = [13,21,141,149]
N = 4
import mx_ref
NC, G = 128, 4
C = np.float32(0.031)
BF = ml_dtypes.bfloat16
def cut(t, i, w=512):
    return t[:, w * i:w * i + w]
def tile(rs):
    return np.stack(rs, axis=2).reshape(128, -1).astype(BF)
def layer(w, X):
    out = []
    for i in range(G):
        for t in range(len(X)):
            p = mx_ref.matmul(mx_ref.quantize(cut(w, len(X) * i + t)), X[t])
            z = p if t == 0 else z + p
        out.append(z)
    return out
def act(Z):
    return [np.maximum(z, 0) * C for z in Z]
def pick(b):
    s = np.zeros((128, 128, 4), np.float32)
    s[np.arange(128), np.arange(128), b] = 1.0
    return mx_ref.quantize(s.reshape(128, 512).astype(BF))
def setup_inputs(rng):
    def f(*shape):
        return mx_ref.flush((rng.standard_normal(shape, dtype=np.float32) * np.exp2(rng.integers(-2, 3, shape[:-1] + (1,)))).astype(BF))
    return {"a": f(N, 128, G * 512), "b": f(N, 128, N * 4 * NC)}
def setup_inputs_blocks(rng):
    d = setup_inputs(rng)
    for k in ("a", "b"): d[k] = mx_ref.spread(d[k], rng, 4)
    return d
def setup_inputs_wide(rng):
    d = setup_inputs(rng)
    for k in ("a", "b"): d[k] = mx_ref.flush((d[k].astype(np.float32) * np.exp2(rng.integers(-8, 9, (N, 1, 1))).astype(np.float32)).astype(BF))
    return d
def reference(a, b):
    S = [pick(t) for t in range(4)]
    y = np.zeros((N, 128, NC, 4), np.float32)
    for c in range(N):
        for r in range(N):
            q = mx_ref.quantize(tile(act(layer(a[r], [mx_ref.quantize(cut(b[r], c, 4 * NC))]))))
            p = np.stack([mx_ref.matmul(S[t], q) for t in range(4)], axis=2)
            y[c] = p if r == 0 else y[c] + p
    return {"y": y.reshape(N, 128, 4 * NC)}

@@ -1,0 +1,230 @@
+from concourse.bass import DstId, RemoteDMATransfer
+from concourse.mybir import dt, AluOpType, ActivationFunctionType
+
+W = 128
+C = 0.031
+SIM_CORES = 256
+
+SCRATCH = {
+    "ab": ("sbuf", [128, 2048], "bfloat16"),
+    "bb": ("sbuf", [128, 2048], "bfloat16"),
+    "aq": ("sbuf", [128, 512], "float8_e4m3fn_x4"),
+    "asc": ("sbuf", [128, 512], "uint8"),
+    "bq": ("sbuf", [128, 512], "float8_e4m3fn_x4"),
+    "bsc": ("sbuf", [128, 512], "uint8"),
+    "e": ("sbuf", [128, 512], "bfloat16"),
+    "sq": ("sbuf", [128, 512], "float8_e4m3fn_x4"),
+    "ss": ("sbuf", [128, 512], "uint8"),
+    "h": ("sbuf", [128, 2048], "bfloat16"),
+    "hq": ("sbuf", [128, 512], "float8_e4m3fn_x4"),
+    "hs": ("sbuf", [128, 512], "uint8"),
+    "rq": ("sbuf", [128, 384], "float8_e4m3fn_x4"),
+    "rs": ("sbuf", [128, 384], "uint8"),
+    "ps": ("psum", [128, 4096], "float32"),
+    "yb": ("sbuf", [128, 512], "float32"),
+}
+SEMAPHORES = ["la0", "la1", "lb0", "lb1", "lb2", "lb3", "aqd", "bqd", "hqd", "mm", "av", "asd", "dd", "cv", "cs", "ys",
+              "ones", "sel", "sqd", "sarr", "relay", "arr0", "arr1", "arr2", "sent"]
+
+
+def _bits(mask):
+    return [k for k in range(16) if (mask >> k) & 1]
+
+
+def _mask(engines):
+    m = 0
+    for k in engines:
+        m |= 1 << k
+    return m
+
+
+def _plan(R, T, topo):
+    others = [d for d in T.cores if d != R]
+    near = [d for d in others if topo.may_write(R, d)]
+    far = [d for d in others if not topo.may_write(R, d)]
+    far.sort(key=lambda d: 0 if topo.host(d) == topo.host(R) else 1)
+    chip = [c for c in range(SIM_CORES)
+            if topo.host(c) == topo.host(R) and topo.chip(c) == topo.chip(R) and c not in T.cores]
+    helpers = []
+    for k, d in enumerate(far):
+        own_die = k == 0
+        helpers.append([c for c in chip if topo.may_write(c, d) and (topo.die(c) == topo.die(R)) == own_die][:2])
+    return {"slots": far + near + [R], "helpers": helpers}
+
+
+def _cols(k):
+    return slice(W * k, W * k + W)
+
+
+def _send(g, T, topo, src, dst, kind, out_k, in_buf, in_k, sem, mask):
+    rid, pid = topo.addr(dst, src)
+    out_buf = {"h": ("rq", "rs"), "r": ("rq", "rs"), "s": ("sq", "ss")}[in_buf][kind]
+    name = {"h": ("hq", "hs"), "r": ("rq", "rs"), "s": ("sq", "ss")}[in_buf][kind]
+    o, i = T[out_buf][:, _cols(out_k)], T[name][:, _cols(in_k)]
+    if kind == 0:
+        o, i = T[out_buf][:, _cols(out_k)].bitcast(dt.uint8), T[name][:, _cols(in_k)].bitcast(dt.uint8)
+    g.remote_dma(o, i, sem, T.sem.sent, pid, rid, mask)
+
+
+def _helper(g, core, T, topo):
+    for R in T.cores:
+        if topo.host(R) != topo.host(core) or topo.chip(R) != topo.chip(core):
+            continue
+        p = _plan(R, T, topo)
+        for k in range(2):
+            for kind in range(2):
+                if p["helpers"][k][kind] != core:
+                    continue
+                j, dst = 2 * k + kind, p["slots"][k]
+                out = topo.mask(core, dst)
+                n = len(_bits(out))
+                g.vector.memset(T.e[:, :], 1.0).then_inc(T.sem.ones, 1)
+                g.wait_ge(T.sem.ones, 1)
+                g.affine_select(T.e[:, :], T.e[:, :], [[-1, 512]], AluOpType.is_equal, 0.0, j, 4).then_inc(T.sem.sel, 1)
+                g.vector.wait_ge(T.sem.sel, 1)
+                g.vector.quantize_mx(T.sq[:, _cols(0)], T.ss[:, _cols(0)], T.e[:, :]).then_inc(T.sem.sqd, 1)
+                g.wait_ge(T.sem.sqd, 1)
+                for part in range(2):
+                    _send(g, T, topo, core, R, part, j, "s", 0, T.sem.sarr, out & topo.mask(core, R))
+                g.wait_ge(T.sem.relay, len(_bits(topo.mask(R, core))[0::2]))
+                _send(g, T, topo, core, dst, kind, k, "r", 0, T.sem["arr%d" % k], out)
+                g.wait_ge(T.sem.sent, 3 * n)
+                return
+
+
+def rank_program(g, core, T, topo):
+    rank = T.rank_of(core)
+    if rank is None:
+        _helper(g, core, T, topo)
+        return
+    S = T.sem
+    V, A, P, Y = g.vector, g.scalar, g.tensor, g.sync
+    p = _plan(core, T, topo)
+    slots, helpers = p["slots"], p["helpers"]
+
+    def tile(buf, k):
+        return buf[:, 512 * k:512 * k + 512]
+
+    def load_b(q, s):
+        r = T.rank_of(slots[s])
+        q.dma_start(tile(T.bb, s), tile(T.b, r)).then_inc(S["lb%d" % s], 16)
+
+    load_b(Y, 0)
+    A.dma_start(T.ab[:, 0:1536], T.a[:, 0:1536]).then_inc(S.la0, 16)
+    Y.dma_start(T.ab[:, 1536:2048], T.a[:, 1536:2048]).then_inc(S.la1, 16)
+    load_b(A, 1)
+    load_b(Y, 2)
+    load_b(A, 3)
+
+    def bank(k):
+        return T.ps[:, 512 * k:512 * k + W]
+
+    def zbank(i, s):
+        return bank(i + 4 * (s % 2))
+
+    def gview(i, s):
+        return T.h[:, 512 * s + i:512 * s + 512:4]
+
+    on_vector = {(i, s): (i == 3 if s == 0 else i % 2 == 1) for s in range(4) for i in range(4)}
+    cnt, done = {"v": 0, "a": 0}, {}
+    for s in range(4):
+        for i in range(4):
+            w = "v" if on_vector[(i, s)] else "a"
+            cnt[w] += 1
+            done[(i, s)] = (w, cnt[w])
+    after = {s: {w: max([done[(i, s)][1] for i in range(4) if done[(i, s)][0] == w]) for w in ("v", "a")} for s in range(4)}
+    sem_of = {"v": S.av, "a": S.asd}
+
+    def quant_b(s):
+        V.wait_ge(S["lb%d" % s], 16)
+        V.quantize_mx(T.bq[:, _cols(s)], T.bsc[:, _cols(s)], tile(T.bb, s)).then_inc(S.bqd, 1)
+
+    def quant_a(i):
+        V.quantize_mx(T.aq[:, _cols(i)], T.asc[:, _cols(i)], tile(T.ab, i)).then_inc(S.aqd, 1)
+
+    def acts(q, w, s):
+        for i in range(4):
+            if done[(i, s)][0] != w:
+                continue
+            q.wait_ge(S.mm, 4 * s + i + 1)
+            if w == "v":
+                V.tensor_scalar(gview(i, s), zbank(i, s), 0.0, C, AluOpType.max, AluOpType.mult).then_inc(S.av, 1)
+            else:
+                A.activation(gview(i, s), zbank(i, s), ActivationFunctionType.Relu, scale=C).then_inc(S.asd, 1)
+
+    def quant_g(s):
+        V.wait_ge(S.av, after[s]["v"])
+        V.wait_ge(S.asd, after[s]["a"])
+        V.quantize_mx(T.hq[:, _cols(s)], T.hs[:, _cols(s)], tile(T.h, s)).then_inc(S.hqd, 1)
+
+    quant_b(0)
+    V.wait_ge(S.la0, 16)
+    for i in range(3):
+        quant_a(i)
+    V.wait_ge(S.la1, 16)
+    quant_a(3)
+    acts(V, "v", 0)
+    quant_g(0)
+    quant_b(1)
+    acts(V, "v", 1)
+    quant_g(1)
+    quant_b(2)
+    quant_b(3)
+    acts(V, "v", 2)
+    quant_g(2)
+    acts(V, "v", 3)
+    quant_g(3)
+    for b in (0, 2):
+        V.wait_ge(S.dd, b + 1)
+        V.tensor_copy(T.yb[:, b:512:4], bank(b)).then_inc(S.cv, 1)
+
+    for s in range(4):
+        acts(A, "a", s)
+    for b in (1, 3):
+        A.wait_ge(S.dd, b + 1)
+        A.activation(T.yb[:, b:512:4], bank(b), ActivationFunctionType.Copy).then_inc(S.cs, 1)
+
+    for s in range(4):
+        P.wait_ge(S.bqd, s + 1)
+        for i in range(4):
+            if s == 0:
+                P.wait_ge(S.aqd, i + 1)
+            if s >= 2:
+                w, n = done[(i, s - 2)]
+                P.wait_ge(sem_of[w], n)
+            P.matmul_mx(zbank(i, s), T.aq[:, _cols(i)], T.asc[:, _cols(i)], T.bq[:, _cols(s)], T.bsc[:, _cols(s)],
+                        True, True).then_inc(S.mm, 1)
+    off = len(_bits(topo.mask(helpers[0][0], slots[0])))
+    P.wait_ge(S.hqd, 4)
+    P.wait_ge(S.av, cnt["v"])
+    P.wait_ge(S.asd, cnt["a"])
+    P.wait_ge(S.sarr, 8 * off)
+    order = [3, 2, 0, 1]
+    for t, s in enumerate(order):
+        if s < 3:
+            P.wait_ge(S["arr%d" % s], 2 * off)
+        q, sc = (T.hq, T.hs) if s == 3 else (T.rq, T.rs)
+        for b in range(4):
+            m = P.matmul_mx(bank(b), T.sq[:, _cols(b)], T.ss[:, _cols(b)], q[:, _cols(s)], sc[:, _cols(s)],
+                            t == 0, t == 3)
+            if t == 3:
+                m.then_inc(S.dd, 1)
+
+    sent = 0
+    for s in range(3):
+        g.wait_ge(S.hqd, s + 1)
+        for kind in range(2):
+            if s < 2:
+                d = helpers[s][kind]
+                m = _mask(_bits(topo.mask(core, d))[0::2])
+                _send(g, T, topo, core, d, kind, 0, "h", s, S.relay, m)
+            else:
+                m = topo.mask(core, slots[s])
+                _send(g, T, topo, core, slots[s], kind, s, "h", s, S.arr2, m)
+            sent += len(_bits(m))
+    g.wait_ge(S.sent, sent)
+
+    Y.wait_ge(S.cv, 2)
+    Y.wait_ge(S.cs, 2)
+    Y.dma_start(T.y[:, :], T.yb[:, :]).then_inc(S.ys, 16)
+    Y.wait_ge(S.ys, 16)

@@ -23,19 +23,13 @@ SCRATCH = {
     "ps": ("psum", [128, 4096], "float32"),
     "yb": ("sbuf", [128, 512], "float32"),
 }
-SEMAPHORES = ["la0", "la1", "lb0", "lb1", "lb2", "lb3", "aqd", "bqd", "hqd", "mm", "av", "asd", "dd", "cv", "cs", "ys",
-              "ones", "sel", "sqd", "sarr", "relay", "arr0", "arr1", "arr2", "sent"]
+SEMAPHORES = ["la0", "la1", "lb0", "lb1", "lb2", "lb3", "aqd", "bqd", "hqd", "mm", "asd", "dd", "cv", "cs", "ys",
+              "ones", "sel", "sqd", "sarr", "relay0", "relay1", "arr0", "arr1", "arr2", "sent"]
+PAIRS = {"h": ("hq", "hs"), "r": ("rq", "rs"), "s": ("sq", "ss")}
 
 
-def _bits(mask):
-    return [k for k in range(16) if (mask >> k) & 1]
-
-
-def _mask(engines):
-    m = 0
-    for k in engines:
-        m |= 1 << k
-    return m
+def _count(mask):
+    return len([k for k in range(16) if (mask >> k) & 1])
 
 
 def _plan(R, T, topo):
@@ -43,27 +37,41 @@ def _plan(R, T, topo):
     near = [d for d in others if topo.may_write(R, d)]
     far = [d for d in others if not topo.may_write(R, d)]
     far.sort(key=lambda d: 0 if topo.host(d) == topo.host(R) else 1)
-    chip = [c for c in range(SIM_CORES)
-            if topo.host(c) == topo.host(R) and topo.chip(c) == topo.chip(R) and c not in T.cores]
-    helpers = []
-    for k, d in enumerate(far):
-        own_die = k == 0
-        helpers.append([c for c in chip if topo.may_write(c, d) and (topo.die(c) == topo.die(R)) == own_die][:2])
-    return {"slots": far + near + [R], "helpers": helpers}
+    owners = [c for c in range(SIM_CORES)
+              if topo.host(c) == topo.host(R) and topo.chip(c) == topo.chip(R) and c not in T.cores
+              and all(topo.may_write(c, d) for d in far)]
+    relays = [[c for c in owners if topo.die(c) == topo.die(R)][0], [c for c in owners if topo.die(c) != topo.die(R)][0]]
+    return {"slots": far + near + [R], "relays": relays, "mine": 2 + sorted([R] + near).index(R)}
 
 
 def _cols(k):
     return slice(W * k, W * k + W)
 
 
-def _send(g, T, topo, src, dst, kind, out_k, in_buf, in_k, sem, mask):
+def _send(g, T, topo, src, dst, kind, in_buf, in_k, out_buf, out_k, sem, mask):
     rid, pid = topo.addr(dst, src)
-    out_buf = {"h": ("rq", "rs"), "r": ("rq", "rs"), "s": ("sq", "ss")}[in_buf][kind]
-    name = {"h": ("hq", "hs"), "r": ("rq", "rs"), "s": ("sq", "ss")}[in_buf][kind]
-    o, i = T[out_buf][:, _cols(out_k)], T[name][:, _cols(in_k)]
+    o, i = T[PAIRS[out_buf][kind]][:, _cols(out_k)], T[PAIRS[in_buf][kind]][:, _cols(in_k)]
     if kind == 0:
-        o, i = T[out_buf][:, _cols(out_k)].bitcast(dt.uint8), T[name][:, _cols(in_k)].bitcast(dt.uint8)
+        o = T[PAIRS[out_buf][kind]][:, _cols(out_k)].bitcast(dt.uint8)
+        i = T[PAIRS[in_buf][kind]][:, _cols(in_k)].bitcast(dt.uint8)
     g.remote_dma(o, i, sem, T.sem.sent, pid, rid, mask)
+    return _count(mask)
+
+
+def _ones_and_zeros(g, T, j):
+    g.vector.memset(T.e[:, :], 1.0).then_inc(T.sem.ones, 1)
+    g.wait_ge(T.sem.ones, 1)
+    g.affine_select(T.e[:, :], T.e[:, :], [[-1, 512]], AluOpType.is_equal, 0.0, j, 4).then_inc(T.sem.sel, 1)
+
+
+def _quant_s(g, T, j):
+    g.vector.wait_ge(T.sem.sel, 1)
+    g.vector.quantize_mx(T.sq[:, _cols(j)], T.ss[:, _cols(j)], T.e[:, :]).then_inc(T.sem.sqd, 1)
+    g.wait_ge(T.sem.sqd, 1)
+
+
+def _s_mask(topo, relay, R, far):
+    return topo.mask(relay, far) & topo.mask(relay, R)
 
 
 def _helper(g, core, T, topo):
@@ -71,25 +79,21 @@ def _helper(g, core, T, topo):
         if topo.host(R) != topo.host(core) or topo.chip(R) != topo.chip(core):
             continue
         p = _plan(R, T, topo)
+        if core not in p["relays"]:
+            continue
+        m = p["relays"].index(core)
+        sent = 0
+        _ones_and_zeros(g, T, m)
+        _quant_s(g, T, m)
+        for part in range(2):
+            sent += _send(g, T, topo, core, R, part, "s", m, "s", m, T.sem.sarr, _s_mask(topo, core, R, p["slots"][0]))
         for k in range(2):
-            for kind in range(2):
-                if p["helpers"][k][kind] != core:
-                    continue
-                j, dst = 2 * k + kind, p["slots"][k]
-                out = topo.mask(core, dst)
-                n = len(_bits(out))
-                g.vector.memset(T.e[:, :], 1.0).then_inc(T.sem.ones, 1)
-                g.wait_ge(T.sem.ones, 1)
-                g.affine_select(T.e[:, :], T.e[:, :], [[-1, 512]], AluOpType.is_equal, 0.0, j, 4).then_inc(T.sem.sel, 1)
-                g.vector.wait_ge(T.sem.sel, 1)
-                g.vector.quantize_mx(T.sq[:, _cols(0)], T.ss[:, _cols(0)], T.e[:, :]).then_inc(T.sem.sqd, 1)
-                g.wait_ge(T.sem.sqd, 1)
-                for part in range(2):
-                    _send(g, T, topo, core, R, part, j, "s", 0, T.sem.sarr, out & topo.mask(core, R))
-                g.wait_ge(T.sem.relay, len(_bits(topo.mask(R, core))[0::2]))
-                _send(g, T, topo, core, dst, kind, k, "r", 0, T.sem["arr%d" % k], out)
-                g.wait_ge(T.sem.sent, 3 * n)
-                return
+            dst = p["slots"][k]
+            g.wait_ge(T.sem["relay%d" % k], _count(topo.mask(R, core)))
+            sent += _send(g, T, topo, core, dst, 0 if m == k else 1, "r", k, "r", k, T.sem["arr%d" % k],
+                          topo.mask(core, dst))
+        g.wait_ge(T.sem.sent, sent)
+        return
 
 
 def rank_program(g, core, T, topo):
@@ -100,7 +104,8 @@ def rank_program(g, core, T, topo):
     S = T.sem
     V, A, P, Y = g.vector, g.scalar, g.tensor, g.sync
     p = _plan(core, T, topo)
-    slots, helpers = p["slots"], p["helpers"]
+    slots, relays, mine = p["slots"], p["relays"], p["mine"]
+    partner = slots[2]
 
     def tile(buf, k):
         return buf[:, 512 * k:512 * k + 512]
@@ -125,16 +130,6 @@ def rank_program(g, core, T, topo):
     def gview(i, s):
         return T.h[:, 512 * s + i:512 * s + 512:4]
 
-    on_vector = {(i, s): (i == 3 if s == 0 else i % 2 == 1) for s in range(4) for i in range(4)}
-    cnt, done = {"v": 0, "a": 0}, {}
-    for s in range(4):
-        for i in range(4):
-            w = "v" if on_vector[(i, s)] else "a"
-            cnt[w] += 1
-            done[(i, s)] = (w, cnt[w])
-    after = {s: {w: max([done[(i, s)][1] for i in range(4) if done[(i, s)][0] == w]) for w in ("v", "a")} for s in range(4)}
-    sem_of = {"v": S.av, "a": S.asd}
-
     def quant_b(s):
         V.wait_ge(S["lb%d" % s], 16)
         V.quantize_mx(T.bq[:, _cols(s)], T.bsc[:, _cols(s)], tile(T.bb, s)).then_inc(S.bqd, 1)
@@ -142,44 +137,33 @@ def rank_program(g, core, T, topo):
     def quant_a(i):
         V.quantize_mx(T.aq[:, _cols(i)], T.asc[:, _cols(i)], tile(T.ab, i)).then_inc(S.aqd, 1)
 
-    def acts(q, w, s):
-        for i in range(4):
-            if done[(i, s)][0] != w:
-                continue
-            q.wait_ge(S.mm, 4 * s + i + 1)
-            if w == "v":
-                V.tensor_scalar(gview(i, s), zbank(i, s), 0.0, C, AluOpType.max, AluOpType.mult).then_inc(S.av, 1)
-            else:
-                A.activation(gview(i, s), zbank(i, s), ActivationFunctionType.Relu, scale=C).then_inc(S.asd, 1)
-
     def quant_g(s):
-        V.wait_ge(S.av, after[s]["v"])
-        V.wait_ge(S.asd, after[s]["a"])
+        V.wait_ge(S.asd, 4 * s + 4)
         V.quantize_mx(T.hq[:, _cols(s)], T.hs[:, _cols(s)], tile(T.h, s)).then_inc(S.hqd, 1)
 
+    sent = 0
+    _ones_and_zeros(g, T, mine)
     quant_b(0)
+    _quant_s(g, T, mine)
+    for kind in range(2):
+        sent += _send(g, T, topo, core, partner, kind, "s", mine, "s", mine, S.sarr, topo.mask(core, partner))
     V.wait_ge(S.la0, 16)
     for i in range(3):
         quant_a(i)
     V.wait_ge(S.la1, 16)
     quant_a(3)
-    acts(V, "v", 0)
-    quant_g(0)
-    quant_b(1)
-    acts(V, "v", 1)
-    quant_g(1)
-    quant_b(2)
-    quant_b(3)
-    acts(V, "v", 2)
-    quant_g(2)
-    acts(V, "v", 3)
-    quant_g(3)
+    for s in range(4):
+        if s < 3:
+            quant_b(s + 1)
+        quant_g(s)
     for b in (0, 2):
         V.wait_ge(S.dd, b + 1)
         V.tensor_copy(T.yb[:, b:512:4], bank(b)).then_inc(S.cv, 1)
 
     for s in range(4):
-        acts(A, "a", s)
+        for i in range(4):
+            A.wait_ge(S.mm, 4 * s + i + 1)
+            A.activation(gview(i, s), zbank(i, s), ActivationFunctionType.Relu, scale=C).then_inc(S.asd, 1)
     for b in (1, 3):
         A.wait_ge(S.dd, b + 1)
         A.activation(T.yb[:, b:512:4], bank(b), ActivationFunctionType.Copy).then_inc(S.cs, 1)
@@ -190,19 +174,18 @@ def rank_program(g, core, T, topo):
             if s == 0:
                 P.wait_ge(S.aqd, i + 1)
             if s >= 2:
-                w, n = done[(i, s - 2)]
-                P.wait_ge(sem_of[w], n)
+                P.wait_ge(S.asd, 4 * (s - 2) + i + 1)
             P.matmul_mx(zbank(i, s), T.aq[:, _cols(i)], T.asc[:, _cols(i)], T.bq[:, _cols(s)], T.bsc[:, _cols(s)],
                         True, True).then_inc(S.mm, 1)
-    off = len(_bits(topo.mask(helpers[0][0], slots[0])))
     P.wait_ge(S.hqd, 4)
-    P.wait_ge(S.av, cnt["v"])
-    P.wait_ge(S.asd, cnt["a"])
-    P.wait_ge(S.sarr, 8 * off)
+    P.wait_ge(S.asd, 16)
+    P.wait_ge(S.sqd, 1)
+    P.wait_ge(S.sarr, 2 * sum(_count(_s_mask(topo, c, core, slots[0])) for c in relays)
+              + 2 * _count(topo.mask(partner, core)))
     order = [3, 2, 0, 1]
     for t, s in enumerate(order):
         if s < 3:
-            P.wait_ge(S["arr%d" % s], 2 * off)
+            P.wait_ge(S["arr%d" % s], 2 * _count(topo.mask(relays[0], slots[0]) if s < 2 else topo.mask(partner, core)))
         q, sc = (T.hq, T.hs) if s == 3 else (T.rq, T.rs)
         for b in range(4):
             m = P.matmul_mx(bank(b), T.sq[:, _cols(b)], T.ss[:, _cols(b)], q[:, _cols(s)], sc[:, _cols(s)],
@@ -210,18 +193,14 @@ def rank_program(g, core, T, topo):
             if t == 3:
                 m.then_inc(S.dd, 1)
 
-    sent = 0
     for s in range(3):
         g.wait_ge(S.hqd, s + 1)
         for kind in range(2):
             if s < 2:
-                d = helpers[s][kind]
-                m = _mask(_bits(topo.mask(core, d))[0::2])
-                _send(g, T, topo, core, d, kind, 0, "h", s, S.relay, m)
+                d = relays[s if kind == 0 else 1 - s]
+                sent += _send(g, T, topo, core, d, kind, "h", s, "r", s, S["relay%d" % s], topo.mask(core, d))
             else:
-                m = topo.mask(core, slots[s])
-                _send(g, T, topo, core, slots[s], kind, s, "h", s, S.arr2, m)
-            sent += len(_bits(m))
+                sent += _send(g, T, topo, core, partner, kind, "h", s, "r", s, S.arr2, topo.mask(core, partner))
     g.wait_ge(S.sent, sent)
 
     Y.wait_ge(S.cv, 2)

from concourse.bass import DstId, RemoteDMATransfer
from concourse.mybir import dt, AluOpType, ActivationFunctionType

W = 128
C = 0.031
SIM_CORES = 256

SCRATCH = {
    "ab": ("sbuf", [128, 2048], "bfloat16"),
    "bb": ("sbuf", [128, 2048], "bfloat16"),
    "aq": ("sbuf", [128, 512], "float8_e4m3fn_x4"),
    "asc": ("sbuf", [128, 512], "uint8"),
    "bq": ("sbuf", [128, 512], "float8_e4m3fn_x4"),
    "bsc": ("sbuf", [128, 512], "uint8"),
    "e": ("sbuf", [128, 512], "bfloat16"),
    "sq": ("sbuf", [128, 512], "float8_e4m3fn_x4"),
    "ss": ("sbuf", [128, 512], "uint8"),
    "h": ("sbuf", [128, 2048], "bfloat16"),
    "hq": ("sbuf", [128, 512], "float8_e4m3fn_x4"),
    "hs": ("sbuf", [128, 512], "uint8"),
    "rq": ("sbuf", [128, 384], "float8_e4m3fn_x4"),
    "rs": ("sbuf", [128, 384], "uint8"),
    "ps": ("psum", [128, 4096], "float32"),
    "yb": ("sbuf", [128, 512], "float32"),
}
SEMAPHORES = ["la0", "la1", "lb0", "lb1", "lb2", "lb3", "aqd", "bqd", "hqd", "mm", "asd", "dd", "cv", "cs", "ys",
              "ones", "sel", "sqd", "sarr", "relay0", "relay1", "arr0", "arr1", "arr2", "sent"]
PAIRS = {"h": ("hq", "hs"), "r": ("rq", "rs"), "s": ("sq", "ss")}


def _count(mask):
    return len([k for k in range(16) if (mask >> k) & 1])


def _plan(R, T, topo):
    others = [d for d in T.cores if d != R]
    near = [d for d in others if topo.may_write(R, d)]
    far = [d for d in others if not topo.may_write(R, d)]
    far.sort(key=lambda d: 0 if topo.host(d) == topo.host(R) else 1)
    owners = [c for c in range(SIM_CORES)
              if topo.host(c) == topo.host(R) and topo.chip(c) == topo.chip(R) and c not in T.cores
              and all(topo.may_write(c, d) for d in far)]
    relays = [[c for c in owners if topo.die(c) == topo.die(R)][0], [c for c in owners if topo.die(c) != topo.die(R)][0]]
    return {"slots": far + near + [R], "relays": relays, "mine": 2 + sorted([R] + near).index(R)}


def _cols(k):
    return slice(W * k, W * k + W)


def _send(g, T, topo, src, dst, kind, in_buf, in_k, out_buf, out_k, sem, mask):
    rid, pid = topo.addr(dst, src)
    o, i = T[PAIRS[out_buf][kind]][:, _cols(out_k)], T[PAIRS[in_buf][kind]][:, _cols(in_k)]
    if kind == 0:
        o = T[PAIRS[out_buf][kind]][:, _cols(out_k)].bitcast(dt.uint8)
        i = T[PAIRS[in_buf][kind]][:, _cols(in_k)].bitcast(dt.uint8)
    g.remote_dma(o, i, sem, T.sem.sent, pid, rid, mask)
    return _count(mask)


def _ones_and_zeros(g, T, j):
    g.vector.memset(T.e[:, :], 1.0).then_inc(T.sem.ones, 1)
    g.wait_ge(T.sem.ones, 1)
    g.affine_select(T.e[:, :], T.e[:, :], [[-1, 512]], AluOpType.is_equal, 0.0, j, 4).then_inc(T.sem.sel, 1)


def _quant_s(g, T, j):
    g.vector.wait_ge(T.sem.sel, 1)
    g.vector.quantize_mx(T.sq[:, _cols(j)], T.ss[:, _cols(j)], T.e[:, :]).then_inc(T.sem.sqd, 1)
    g.wait_ge(T.sem.sqd, 1)


def _s_mask(topo, relay, R, far):
    return topo.mask(relay, far) & topo.mask(relay, R)


def _helper(g, core, T, topo):
    for R in T.cores:
        if topo.host(R) != topo.host(core) or topo.chip(R) != topo.chip(core):
            continue
        p = _plan(R, T, topo)
        if core not in p["relays"]:
            continue
        m = p["relays"].index(core)
        sent = 0
        _ones_and_zeros(g, T, m)
        _quant_s(g, T, m)
        for part in range(2):
            sent += _send(g, T, topo, core, R, part, "s", m, "s", m, T.sem.sarr, _s_mask(topo, core, R, p["slots"][0]))
        for k in range(2):
            dst = p["slots"][k]
            g.wait_ge(T.sem["relay%d" % k], _count(topo.mask(R, core)))
            sent += _send(g, T, topo, core, dst, 0 if m == k else 1, "r", k, "r", k, T.sem["arr%d" % k],
                          topo.mask(core, dst))
        g.wait_ge(T.sem.sent, sent)
        return


def rank_program(g, core, T, topo):
    rank = T.rank_of(core)
    if rank is None:
        _helper(g, core, T, topo)
        return
    S = T.sem
    V, A, P, Y = g.vector, g.scalar, g.tensor, g.sync
    p = _plan(core, T, topo)
    slots, relays, mine = p["slots"], p["relays"], p["mine"]
    partner = slots[2]

    def tile(buf, k):
        return buf[:, 512 * k:512 * k + 512]

    def load_b(q, s):
        r = T.rank_of(slots[s])
        q.dma_start(tile(T.bb, s), tile(T.b, r)).then_inc(S["lb%d" % s], 16)

    load_b(Y, 0)
    A.dma_start(T.ab[:, 0:1536], T.a[:, 0:1536]).then_inc(S.la0, 16)
    Y.dma_start(T.ab[:, 1536:2048], T.a[:, 1536:2048]).then_inc(S.la1, 16)
    load_b(A, 1)
    load_b(Y, 2)
    load_b(A, 3)

    def bank(k):
        return T.ps[:, 512 * k:512 * k + W]

    def zbank(i, s):
        return bank(i + 4 * (s % 2))

    def gview(i, s):
        return T.h[:, 512 * s + i:512 * s + 512:4]

    def quant_b(s):
        V.wait_ge(S["lb%d" % s], 16)
        V.quantize_mx(T.bq[:, _cols(s)], T.bsc[:, _cols(s)], tile(T.bb, s)).then_inc(S.bqd, 1)

    def quant_a(i):
        V.quantize_mx(T.aq[:, _cols(i)], T.asc[:, _cols(i)], tile(T.ab, i)).then_inc(S.aqd, 1)

    def quant_g(s):
        V.wait_ge(S.asd, 4 * s + 4)
        V.quantize_mx(T.hq[:, _cols(s)], T.hs[:, _cols(s)], tile(T.h, s)).then_inc(S.hqd, 1)

    sent = 0
    _ones_and_zeros(g, T, mine)
    quant_b(0)
    _quant_s(g, T, mine)
    for kind in range(2):
        sent += _send(g, T, topo, core, partner, kind, "s", mine, "s", mine, S.sarr, topo.mask(core, partner))
    V.wait_ge(S.la0, 16)
    for i in range(3):
        quant_a(i)
    V.wait_ge(S.la1, 16)
    quant_a(3)
    for s in range(4):
        if s < 3:
            quant_b(s + 1)
        quant_g(s)
    for b in (0, 2):
        V.wait_ge(S.dd, b + 1)
        V.tensor_copy(T.yb[:, b:512:4], bank(b)).then_inc(S.cv, 1)

    for s in range(4):
        for i in range(4):
            A.wait_ge(S.mm, 4 * s + i + 1)
            A.activation(gview(i, s), zbank(i, s), ActivationFunctionType.Relu, scale=C).then_inc(S.asd, 1)
    for b in (1, 3):
        A.wait_ge(S.dd, b + 1)
        A.activation(T.yb[:, b:512:4], bank(b), ActivationFunctionType.Copy).then_inc(S.cs, 1)

    for s in range(4):
        P.wait_ge(S.bqd, s + 1)
        for i in range(4):
            if s == 0:
                P.wait_ge(S.aqd, i + 1)
            if s >= 2:
                P.wait_ge(S.asd, 4 * (s - 2) + i + 1)
            P.matmul_mx(zbank(i, s), T.aq[:, _cols(i)], T.asc[:, _cols(i)], T.bq[:, _cols(s)], T.bsc[:, _cols(s)],
                        True, True).then_inc(S.mm, 1)
    P.wait_ge(S.hqd, 4)
    P.wait_ge(S.asd, 16)
    P.wait_ge(S.sqd, 1)
    P.wait_ge(S.sarr, 2 * sum(_count(_s_mask(topo, c, core, slots[0])) for c in relays)
              + 2 * _count(topo.mask(partner, core)))
    order = [3, 2, 0, 1]
    for t, s in enumerate(order):
        if s < 3:
            P.wait_ge(S["arr%d" % s], 2 * _count(topo.mask(relays[0], slots[0]) if s < 2 else topo.mask(partner, core)))
        q, sc = (T.hq, T.hs) if s == 3 else (T.rq, T.rs)
        for b in range(4):
            m = P.matmul_mx(bank(b), T.sq[:, _cols(b)], T.ss[:, _cols(b)], q[:, _cols(s)], sc[:, _cols(s)],
                            t == 0, t == 3)
            if t == 3:
                m.then_inc(S.dd, 1)

    for s in range(3):
        g.wait_ge(S.hqd, s + 1)
        for kind in range(2):
            if s < 2:
                d = relays[s if kind == 0 else 1 - s]
                sent += _send(g, T, topo, core, d, kind, "h", s, "r", s, S["relay%d" % s], topo.mask(core, d))
            else:
                sent += _send(g, T, topo, core, partner, kind, "h", s, "r", s, S.arr2, topo.mask(core, partner))
    g.wait_ge(S.sent, sent)

    Y.wait_ge(S.cv, 2)
    Y.wait_ge(S.cs, 2)
    Y.dma_start(T.y[:, :], T.yb[:, :]).then_inc(S.ys, 16)
    Y.wait_ge(S.ys, 16)
